import numpy as np
import ml_dtypes


def mxq(x, axis, fmt="e4m3"):
    dtype, down = {"e4m3": (ml_dtypes.float8_e4m3fn, 7), "e5m2": (ml_dtypes.float8_e5m2, 14)}[fmt]
    v = np.moveaxis(np.asarray(x, np.float32).astype(ml_dtypes.bfloat16).astype(np.float64), axis, -1)
    blocks = v.reshape(v.shape[:-1] + (-1, 32))
    amax = np.abs(blocks).max(-1, keepdims=True)
    byte = np.maximum(np.where(amax > 0, np.frexp(amax)[1] - 1 + 127, 0) - down, 1)
    scale = np.exp2(byte - 127.0)
    codes = (blocks / scale).astype(np.float32).astype(dtype).astype(np.float64)
    return np.moveaxis((codes * scale).reshape(v.shape), -1, axis)


WIDE = False


def mx_kscale(k):
    if not WIDE:
        return np.ones(k)
    levels = np.array([10, -10, 5, -5, 0])
    if k % 512:
        return np.exp2(np.random.permutation(np.resize(levels, k // 32))).repeat(32)
    a = np.empty((k // 512, 16))
    for p in range(k // 512):
        a[p, :8] = np.random.permutation(np.resize(levels, 8))
        for g in range(8):
            far = levels[np.abs(levels - a[p, g]) >= 10]
            a[p, g + 8] = far[np.random.randint(len(far))]
    return np.exp2(a.ravel()).repeat(32)


def f64(x):
    return np.asarray(x).astype(np.float64)


def striped(idx):
    return np.tile(idx.reshape(-1, 16).T, (8, 1)).astype(np.uint16)


def unstriped(offs):
    return offs[:16].T.reshape(-1).astype(np.int64)


def pack_weight(w):
    k, n = w.shape
    w = f64(np.asarray(w, np.float32).astype(ml_dtypes.bfloat16)).reshape(k // 32, 32, n)
    amax = np.abs(w).max(1)
    byte = np.clip(np.where(amax > 0, np.frexp(amax)[1] - 1 + 127 - 7, 1), 1, 254)
    scaled = (w * np.exp2(127.0 - byte)[:, None, :]).reshape(k, n).astype(np.float32)
    words = np.ascontiguousarray(scaled.reshape(k // 512, 128, 4, n).transpose(0, 1, 3, 2)).astype(ml_dtypes.float8_e4m3fn).view(np.uint8)
    return words, np.ascontiguousarray(byte.astype(np.uint8).reshape(k // 512, 16, n))


def unpack_weight(words, scales):
    g, p, n, _ = words.shape
    vals = np.ascontiguousarray(words).view(ml_dtypes.float8_e4m3fn).astype(np.float64) * np.repeat(np.exp2(scales.astype(np.float64) - 127.0), 8, axis=1)[..., None]
    return vals.transpose(0, 1, 3, 2).reshape(g * 512, n)


K, T, S, N, H = 512, 1024, 512, 256, 512


def setup_inputs():
    n = np.random.standard_normal
    s = mx_kscale(K)[:, None]
    u = mx_kscale(H)
    packed_xT = pack_weight(n((K, T)) * s)
    return {
        "x_words": packed_xT[0],
        "x_scales": packed_xT[1],
        "hT": (n((K, H)) / np.sqrt(K) / s).astype(np.float32),
        "spk": (np.floor(np.random.uniform(0.0, 4.0, (H, S)))).astype(np.float32),
        "unit": (np.random.uniform(0.6, 1.4, (H, 1)) * u[:, None]).astype(np.float32),
        "w1": (n((H, N)) / np.sqrt(H) / u[:, None]).astype(np.float32),
        "offs": striped(np.random.permutation(T)[:S]),
        "nb": striped(np.random.permutation(S)),
    }


def reference(x_words, x_scales, hT, spk, unit, w1, offs, nb):
    hTq = mxq(f64(hT), 0, "e4m3")
    xq = unpack_weight(x_words, x_scales)[:, unstriped(offs)]
    y = hTq.T @ xq
    rate = np.exp(1.0 * np.tanh(y))
    ll = f64(spk) * np.log(rate) - rate
    dev = (f64(spk) - rate) / np.sqrt(rate)
    hid = f64(unit) * (ll + dev[:, unstriped(nb)])
    return mxq(f64(w1), 0, "e4m3").T @ mxq(hid, 0, "e4m3")

@@ -1,0 +1,239 @@
+from contextlib import ExitStack
+
+import concourse.mybir as mybir
+from concourse.masks import make_identity
+
+K, T, S, N, H = 512, 1024, 512, 256, 512
+FLOPS = 2 * K * H * S + 2 * H * N * S
+
+F32 = mybir.dt.float32
+BF16 = mybir.dt.bfloat16
+I32 = mybir.dt.int32
+U32 = mybir.dt.uint32
+U16 = mybir.dt.uint16
+U8 = mybir.dt.uint8
+FP8X4 = mybir.dt.float8_e4m3fn_x4
+ACT = mybir.ActivationFunctionType
+ALU = mybir.AluOpType
+
+P = 128
+PACK = 4
+TILES = H // P
+CHUNKS = S // P
+HALF = S // 2
+HALF_COLS = HALF // 16
+
+
+def interleave(copy, grouped, raw):
+    copy(
+        grouped[:].rearrange("p (c i) r -> p c r i", i=4),
+        raw.rearrange("p r (c i) -> p c r i", i=4),
+    )
+
+
+def tile_picked_yplcel_ll_p_kernel(
+    tc, x_words, x_scales, hT, spk, unit, w1, offs, nb, out
+):
+    nc = tc.nc
+    with ExitStack() as ctx:
+        keep = ctx.enter_context(tc.tile_pool(name="keep", bufs=1))
+        sums = ctx.enter_context(tc.psum_pool(name="sums", bufs=1))
+        banks = ctx.enter_context(tc.psum_pool(name="banks", bufs=4))
+
+        def sbuf(name, shape, dtype):
+            return keep.tile(shape, dtype, name=name, align_bytes=64)
+
+        offs_t = keep.tile([P, S // 16], U16, name="offs_t")
+        nb_t = keep.tile([P, S // 16], U16, name="nb_t")
+        xs = sbuf("xs", [P, T], U8)
+        xw = sbuf("xw", [P, T], U32)
+        hT_rows = hT.rearrange("(p r) c -> p r c", r=PACK)
+        h_raw = [sbuf(f"h_raw{t}", [P, PACK, P], F32) for t in range(TILES)]
+        spk_t = [sbuf(f"spk{t}", [P, S], F32) for t in range(TILES)]
+        u_t = sbuf("u_t", [P, PACK], F32)
+        w_raw = sbuf("w_raw", [P, PACK, N], F32)
+
+        def load_positions(t):
+            nc.sync.dma_start(h_raw[t][:], hT_rows[:, :, P * t : P * (t + 1)])
+
+        def load_counts(t):
+            nc.sync.dma_start(spk_t[t][:], spk[P * t : P * (t + 1), :])
+
+        nc.gpsimd.memset(xs[:].bitcast(I32), 0)
+        nc.sync.dma_start(offs_t[:], offs)
+        nc.sync.dma_start(u_t[:], unit.rearrange("(p r) o -> p (r o)", r=PACK))
+        for q in range(4):
+            nc.sync.dma_start(
+                xs[32 * q : 32 * q + 4, :].bitcast(I32),
+                x_scales[0, 4 * q : 4 * q + 4, :].bitcast(I32),
+            )
+        load_positions(0)
+        nc.sync.dma_start(
+            xw[:].bitcast(I32), x_words[0].rearrange("p n r -> p (n r)").bitcast(I32)
+        )
+        load_positions(1)
+        load_counts(0)
+        load_positions(2)
+        load_positions(3)
+        for t in range(1, TILES):
+            load_counts(t)
+        nc.sync.dma_start(nb_t[:], nb)
+        nc.sync.dma_start(w_raw[:], w1.rearrange("(p r) n -> p r n", r=PACK))
+
+        ident = sbuf("ident", [P, P], F32)
+        make_identity(nc, ident[:])
+
+        gs = sbuf("gs", [P, S], U8)
+        nc.vector.tensor_copy(gs[:], xs[:].indirect(offs_t[:]))
+        gw = [sbuf(f"gw{h}", [P, HALF], U32) for h in range(2)]
+
+        h_bf = [sbuf(f"h_bf{t}", [P, P, PACK], BF16) for t in range(TILES)]
+        h_codes = [sbuf(f"h_codes{t}", [P, P], U32) for t in range(TILES)]
+        h_scales = [sbuf(f"h_scales{t}", [P, P], U8) for t in range(TILES)]
+
+        def quantize(codes, scales, grouped):
+            nc.vector.quantize_mx(
+                out=codes[:].bitcast(FP8X4),
+                scales=scales[:],
+                in_=grouped[:].rearrange("p c r -> p (c r)"),
+            )
+
+        def gather_words(h):
+            nc.vector.tensor_copy(
+                gw[h][:], xw[:].indirect(offs_t[:, HALF_COLS * h : HALF_COLS * (h + 1)])
+            )
+
+        interleave(nc.vector.tensor_copy, h_bf[0], h_raw[0][:])
+        quantize(h_codes[0], h_scales[0], h_bf[0])
+        gather_words(0)
+        gather_words(1)
+
+        ub = banks.tile([P, H], F32, name="ub", tag="bank")
+        for r in range(PACK):
+            nc.tensor.transpose(
+                ub[:, P * r : P * (r + 1)], u_t[:, r : r + 1].to_broadcast([P, P]), ident[:]
+            )
+        nunit = sbuf("nunit", [P, H], F32)
+        nc.scalar.activation(
+            nunit[:].rearrange("p (u m e) -> p u m e", u=2, e=2),
+            ub[:].rearrange("p (u e m) -> p u m e", u=2, e=2),
+            ACT.Copy, scale=-1.0,
+        )
+
+        acc = [sums.tile([P, H], F32, name=f"acc{c}") for c in range(CHUNKS)]
+        ntanh = [sbuf(f"ntanh{t}", [P, S], F32) for t in range(TILES)]
+        rate = [sbuf(f"rate{t}", [P, S], F32) for t in range(TILES)]
+        rsq = [sbuf(f"rsq{t}", [P, S], F32) for t in range(TILES)]
+        gap = [sbuf(f"gap{t}", [P, S], F32) for t in range(TILES)]
+        ndev = [sbuf(f"ndev{t}", [P, S], F32) for t in range(TILES)]
+        nprod = [sbuf(f"nprod{t}", [P, S], F32) for t in range(TILES)]
+        fetched = [[sbuf(f"fetched{t}_{h}", [P, HALF], F32) for h in range(2)] for t in range(TILES)]
+
+        def add_turned(c, t, src, start=False, stop=False):
+            nc.tensor.matmul(
+                acc[c][:, P * t : P * (t + 1)], src, ident[:],
+                start=start, stop=stop, is_transpose=True,
+            )
+
+        def scores(t):
+            y = banks.tile([P, S], F32, name="y", tag="bank")
+            for h in range(2):
+                cols = slice(HALF * h, HALF * (h + 1))
+                nc.tensor.matmul_mx(
+                    out=y[:, cols],
+                    lhsT=h_codes[t][:].bitcast(FP8X4), lhsT_scale=h_scales[t][:],
+                    rhs=gw[h][:].bitcast(FP8X4), rhs_scale=gs[:, cols],
+                    start=True, stop=True,
+                )
+                if t == 0:
+                    rates(t, y, cols)
+            if t > 0:
+                rates(t, y, slice(0, S))
+
+        def rates(t, y, cols):
+            nc.scalar.activation(ntanh[t][:, cols], y[:, cols], ACT.Tanh, scale=-1.0)
+            nc.scalar.activation(rate[t][:, cols], ntanh[t][:, cols], ACT.Exp, scale=-1.0)
+            nc.scalar.activation(rsq[t][:, cols], ntanh[t][:, cols], ACT.Exp, scale=0.5)
+
+        def prepare(t, copy):
+            interleave(copy, h_bf[t], h_raw[t][:])
+            quantize(h_codes[t], h_scales[t], h_bf[t])
+
+        def residuals(t):
+            nc.vector.tensor_tensor(gap[t][:], rate[t][:], spk_t[t][:], ALU.subtract)
+            nc.vector.tensor_tensor(ndev[t][:], gap[t][:], rsq[t][:], ALU.mult)
+
+        def likelihood(t):
+            nc.vector.tensor_tensor(nprod[t][:], ntanh[t][:], spk_t[t][:], ALU.mult)
+            for c in range(CHUNKS):
+                add_turned(c, t, rate[t][:, P * c : P * (c + 1)], start=(t == 0))
+            for c in range(CHUNKS):
+                add_turned(c, t, nprod[t][:, P * c : P * (c + 1)])
+
+        scores(0)
+        for t in range(1, TILES):
+            prepare(t, nc.scalar.copy if t == 1 else nc.vector.tensor_copy)
+            scores(t)
+        for t in range(TILES):
+            residuals(t)
+            likelihood(t)
+
+        w_bf = sbuf("w_bf", [P, N, PACK], BF16)
+        w_codes = sbuf("w_codes", [P, N], U32)
+        w_scales = sbuf("w_scales", [P, N], U8)
+
+        def fetch(t, h):
+            window = ndev[t][:].indirect(nb_t[:, HALF_COLS * h : HALF_COLS * (h + 1)])
+            if (t, h) == (TILES - 1, 0):
+                nc.vector.tensor_copy(fetched[t][h][:], window)
+            else:
+                nc.scalar.activation(fetched[t][h][:], window, ACT.Copy)
+            for cc in range(2):
+                add_turned(2 * h + cc, t, fetched[t][h][:, P * cc : P * (cc + 1)], stop=(t == TILES - 1))
+
+        def finish(h):
+            words = banks.tile([P, 2, 2, P], F32, name="words", tag="bank")
+            for cc in range(2):
+                c = 2 * h + cc
+                hid_t = sbuf(f"hid_t{c}", [P, H], BF16)
+                nc.vector.tensor_tensor(
+                    hid_t[:].rearrange("p (u m e) -> p u m e", u=2, e=2),
+                    acc[c][:].rearrange("p (m u e) -> p u m e", u=2, e=2),
+                    nunit[:].rearrange("p (u m e) -> p u m e", u=2, e=2),
+                    ALU.mult,
+                )
+                for u in range(2):
+                    nc.tensor.transpose(
+                        words[:, cc, u, :], hid_t[:].bitcast(F32)[:, P * u : P * (u + 1)], ident[:]
+                    )
+            hid_bf = sbuf(f"hid_bf{h}", [P, HALF, PACK], BF16)
+            nc.scalar.copy(
+                hid_bf[:].rearrange("p j r -> p (j r)").bitcast(F32).rearrange("p (c j u) -> p c j u", c=2, u=2),
+                words[:].rearrange("p c u j -> p c j u"),
+            )
+            hid_codes = sbuf(f"hid_codes{h}", [P, HALF], U32)
+            hid_scales = sbuf(f"hid_scales{h}", [P, HALF], U8)
+            quantize(hid_codes, hid_scales, hid_bf)
+            res = banks.tile([P, 2, HALF], F32, name="res", tag="bank")
+            for a in range(2):
+                nc.tensor.matmul_mx(
+                    out=res[:, a, :],
+                    lhsT=w_codes[:, P * a : P * (a + 1)].bitcast(FP8X4),
+                    lhsT_scale=w_scales[:, P * a : P * (a + 1)],
+                    rhs=hid_codes[:].bitcast(FP8X4), rhs_scale=hid_scales[:],
+                    start=True, stop=True,
+                )
+            staged = sbuf(f"staged{h}", [P, 2, HALF], F32)
+            nc.scalar.copy(staged[:], res[:])
+            nc.sync.dma_start(
+                out.rearrange("(a p) j -> p a j", a=2)[:, :, HALF * h : HALF * (h + 1)], staged[:]
+            )
+
+        for t in range(TILES):
+            fetch(t, 0)
+        interleave(nc.vector.tensor_copy, w_bf, w_raw[:])
+        quantize(w_codes, w_scales, w_bf)
+        for t in range(TILES):
+            fetch(t, 1)
+        finish(0)
+        finish(1)

@@ -1,7 +1,6 @@
 from contextlib import ExitStack
 
 import concourse.mybir as mybir
-from concourse.masks import make_identity
 
 K, T, S, N, H = 512, 1024, 512, 256, 512
 FLOPS = 2 * K * H * S + 2 * H * N * S
@@ -18,8 +17,6 @@ ALU = mybir.AluOpType
 
 P = 128
 PACK = 4
-TILES = H // P
-CHUNKS = S // P
 HALF = S // 2
 HALF_COLS = HALF // 16
 
@@ -27,7 +24,7 @@ HALF_COLS = HALF // 16
 def interleave(copy, grouped, raw):
     copy(
         grouped[:].rearrange("p (c i) r -> p c r i", i=4),
-        raw.rearrange("p r (c i) -> p c r i", i=4),
+        raw[:].rearrange("p r (c i) -> p c r i", i=4),
     )
 
 
@@ -37,111 +34,93 @@ def tile_picked_yplcel_ll_p_kernel(
     nc = tc.nc
     with ExitStack() as ctx:
         keep = ctx.enter_context(tc.tile_pool(name="keep", bufs=1))
-        sums = ctx.enter_context(tc.psum_pool(name="sums", bufs=1))
-        banks = ctx.enter_context(tc.psum_pool(name="banks", bufs=4))
+        banks = ctx.enter_context(tc.psum_pool(name="banks", bufs=1))
 
         def sbuf(name, shape, dtype):
             return keep.tile(shape, dtype, name=name, align_bytes=64)
 
+        def quantize(codes, scales, grouped):
+            nc.vector.quantize_mx(out=codes.bitcast(FP8X4), scales=scales, in_=grouped)
+
         offs_t = keep.tile([P, S // 16], U16, name="offs_t")
         nb_t = keep.tile([P, S // 16], U16, name="nb_t")
         xs = sbuf("xs", [P, T], U8)
-        xw = sbuf("xw", [P, T], U32)
-        hT_rows = hT.rearrange("(p r) c -> p r c", r=PACK)
-        h_raw = [sbuf(f"h_raw{t}", [P, PACK, P], F32) for t in range(TILES)]
-        spk_t = [sbuf(f"spk{t}", [P, S], F32) for t in range(TILES)]
+        xw = keep.tile([P, T], U32, name="xw", tag="words", align_bytes=64)
+        h_raw = [sbuf(f"h_raw{a}", [P, PACK, H // 2], F32) for a in range(2)]
+        spk_t = [sbuf(f"spk{t}", [P, S], F32) for t in range(PACK)]
         u_t = sbuf("u_t", [P, PACK], F32)
         w_raw = sbuf("w_raw", [P, PACK, N], F32)
-
-        def load_positions(t):
-            nc.sync.dma_start(h_raw[t][:], hT_rows[:, :, P * t : P * (t + 1)])
-
-        def load_counts(t):
-            nc.sync.dma_start(spk_t[t][:], spk[P * t : P * (t + 1), :])
+        hT_rows = hT.rearrange("(p r) c -> p r c", r=PACK)
+        spk_rows = spk.rearrange("(p t) j -> p t j", t=PACK)
 
         nc.gpsimd.memset(xs[:].bitcast(I32), 0)
         nc.sync.dma_start(offs_t[:], offs)
-        nc.sync.dma_start(u_t[:], unit.rearrange("(p r) o -> p (r o)", r=PACK))
         for q in range(4):
             nc.sync.dma_start(
                 xs[32 * q : 32 * q + 4, :].bitcast(I32),
                 x_scales[0, 4 * q : 4 * q + 4, :].bitcast(I32),
             )
-        load_positions(0)
+        for a in range(2):
+            nc.sync.dma_start(h_raw[a][:], hT_rows[:, :, H // 2 * a : H // 2 * (a + 1)])
         nc.sync.dma_start(
             xw[:].bitcast(I32), x_words[0].rearrange("p n r -> p (n r)").bitcast(I32)
         )
-        load_positions(1)
-        load_counts(0)
-        load_positions(2)
-        load_positions(3)
-        for t in range(1, TILES):
-            load_counts(t)
-        nc.sync.dma_start(nb_t[:], nb)
         nc.sync.dma_start(w_raw[:], w1.rearrange("(p r) n -> p r n", r=PACK))
-
-        ident = sbuf("ident", [P, P], F32)
-        make_identity(nc, ident[:])
+        nc.sync.dma_start(spk_t[0][:], spk_rows[:, 0, :])
+        nc.sync.dma_start(u_t[:], unit.rearrange("(p t) o -> p (t o)", t=PACK))
+        for t in range(1, PACK):
+            nc.sync.dma_start(spk_t[t][:], spk_rows[:, t, :])
+        nc.sync.dma_start(nb_t[:], nb)
 
         gs = sbuf("gs", [P, S], U8)
-        nc.vector.tensor_copy(gs[:], xs[:].indirect(offs_t[:]))
         gw = [sbuf(f"gw{h}", [P, HALF], U32) for h in range(2)]
+        h_bf = sbuf("h_bf", [P, PACK, P, PACK], BF16)
+        first_codes = sbuf("first_codes", [P, P], U32)
+        first_scales = sbuf("first_scales", [P, P], U8)
 
-        h_bf = [sbuf(f"h_bf{t}", [P, P, PACK], BF16) for t in range(TILES)]
-        h_codes = [sbuf(f"h_codes{t}", [P, P], U32) for t in range(TILES)]
-        h_scales = [sbuf(f"h_scales{t}", [P, P], U8) for t in range(TILES)]
-
-        def quantize(codes, scales, grouped):
-            nc.vector.quantize_mx(
-                out=codes[:].bitcast(FP8X4),
-                scales=scales[:],
-                in_=grouped[:].rearrange("p c r -> p (c r)"),
+        nc.vector.tensor_copy(gs[:], xs[:].indirect(offs_t[:]))
+        for a, copy in enumerate((nc.scalar.copy, nc.vector.tensor_copy)):
+            copy(
+                h_bf[:, :, P // 2 * a : P // 2 * (a + 1), :].rearrange("p t m r -> p m r t"),
+                h_raw[a][:].rearrange("p r (m t) -> p m r t", t=PACK),
             )
-
-        def gather_words(h):
+        quantize(first_codes[:], first_scales[:], h_bf[:, 0].rearrange("p m r -> p (m r)"))
+        for h in range(2):
             nc.vector.tensor_copy(
                 gw[h][:], xw[:].indirect(offs_t[:, HALF_COLS * h : HALF_COLS * (h + 1)])
             )
+        rest_codes = keep.tile([P, H - P], U32, name="rest_codes", tag="words", align_bytes=64)
+        rest_scales = sbuf("rest_scales", [P, H - P], U8)
+        quantize(rest_codes[:], rest_scales[:], h_bf[:, 1:].rearrange("p t m r -> p (t m r)"))
+        h_codes = [first_codes[:]] + [rest_codes[:, P * t : P * (t + 1)] for t in range(PACK - 1)]
+        h_scales = [first_scales[:]] + [rest_scales[:, P * t : P * (t + 1)] for t in range(PACK - 1)]
 
-        interleave(nc.vector.tensor_copy, h_bf[0], h_raw[0][:])
-        quantize(h_codes[0], h_scales[0], h_bf[0])
-        gather_words(0)
-        gather_words(1)
+        w_bf = sbuf("w_bf", [P, N, PACK], BF16)
+        w_codes = sbuf("w_codes", [P, N], U32)
+        w_scales = sbuf("w_scales", [P, N], U8)
+        interleave(nc.vector.tensor_copy, w_bf, w_raw)
+        quantize(w_codes[:], w_scales[:], w_bf[:].rearrange("p n r -> p (n r)"))
 
-        ub = banks.tile([P, H], F32, name="ub", tag="bank")
-        for r in range(PACK):
-            nc.tensor.transpose(
-                ub[:, P * r : P * (r + 1)], u_t[:, r : r + 1].to_broadcast([P, P]), ident[:]
-            )
-        nunit = sbuf("nunit", [P, H], F32)
-        nc.scalar.activation(
-            nunit[:].rearrange("p (u m e) -> p u m e", u=2, e=2),
-            ub[:].rearrange("p (u e m) -> p u m e", u=2, e=2),
-            ACT.Copy, scale=-1.0,
-        )
+        tanh = [sbuf(f"tanh{t}", [P, S], F32) for t in range(PACK)]
+        rate = [sbuf(f"rate{t}", [P, S], F32) for t in range(PACK)]
+        rsq = [sbuf(f"rsq{t}", [P, S], F32) for t in range(PACK)]
+        gap = [sbuf(f"gap{t}", [P, S], F32) for t in range(PACK)]
+        dev = [sbuf(f"dev{t}", [P, S], F32) for t in range(PACK)]
+        prod = [sbuf(f"prod{t}", [P, S], F32) for t in range(PACK)]
+        nll = sbuf("nll", [P, PACK, S], F32)
 
-        acc = [sums.tile([P, H], F32, name=f"acc{c}") for c in range(CHUNKS)]
-        ntanh = [sbuf(f"ntanh{t}", [P, S], F32) for t in range(TILES)]
-        rate = [sbuf(f"rate{t}", [P, S], F32) for t in range(TILES)]
-        rsq = [sbuf(f"rsq{t}", [P, S], F32) for t in range(TILES)]
-        gap = [sbuf(f"gap{t}", [P, S], F32) for t in range(TILES)]
-        ndev = [sbuf(f"ndev{t}", [P, S], F32) for t in range(TILES)]
-        nprod = [sbuf(f"nprod{t}", [P, S], F32) for t in range(TILES)]
-        fetched = [[sbuf(f"fetched{t}_{h}", [P, HALF], F32) for h in range(2)] for t in range(TILES)]
+        def rates(t, y, cols):
+            nc.scalar.activation(tanh[t][:, cols], y[:, cols], ACT.Tanh)
+            nc.scalar.activation(rate[t][:, cols], tanh[t][:, cols], ACT.Exp)
+            nc.scalar.activation(rsq[t][:, cols], tanh[t][:, cols], ACT.Exp, scale=-0.5)
 
-        def add_turned(c, t, src, start=False, stop=False):
-            nc.tensor.matmul(
-                acc[c][:, P * t : P * (t + 1)], src, ident[:],
-                start=start, stop=stop, is_transpose=True,
-            )
-
-        def scores(t):
-            y = banks.tile([P, S], F32, name="y", tag="bank")
+        for t in range(PACK):
+            y = banks.tile([P, S], F32, name=f"y{t}")
             for h in range(2):
                 cols = slice(HALF * h, HALF * (h + 1))
                 nc.tensor.matmul_mx(
                     out=y[:, cols],
-                    lhsT=h_codes[t][:].bitcast(FP8X4), lhsT_scale=h_scales[t][:],
+                    lhsT=h_codes[t].bitcast(FP8X4), lhsT_scale=h_scales[t],
                     rhs=gw[h][:].bitcast(FP8X4), rhs_scale=gs[:, cols],
                     start=True, stop=True,
                 )
@@ -150,71 +129,33 @@ def tile_picked_yplcel_ll_p_kernel(
             if t > 0:
                 rates(t, y, slice(0, S))
 
-        def rates(t, y, cols):
-            nc.scalar.activation(ntanh[t][:, cols], y[:, cols], ACT.Tanh, scale=-1.0)
-            nc.scalar.activation(rate[t][:, cols], ntanh[t][:, cols], ACT.Exp, scale=-1.0)
-            nc.scalar.activation(rsq[t][:, cols], ntanh[t][:, cols], ACT.Exp, scale=0.5)
+        for t in range(PACK):
+            u = u_t[:, t : t + 1]
+            nc.vector.scalar_tensor_tensor(prod[t][:], tanh[t][:], u, spk_t[t][:], ALU.mult, ALU.mult)
+            nc.vector.tensor_tensor(gap[t][:], spk_t[t][:], rate[t][:], ALU.subtract)
+            nc.vector.scalar_tensor_tensor(nll[:, t, :], rate[t][:], u, prod[t][:], ALU.mult, ALU.subtract)
+            nc.vector.scalar_tensor_tensor(dev[t][:], gap[t][:], u, rsq[t][:], ALU.mult, ALU.mult)
 
-        def prepare(t, copy):
-            interleave(copy, h_bf[t], h_raw[t][:])
-            quantize(h_codes[t], h_scales[t], h_bf[t])
+        fetched = [sbuf(f"fetched{h}", [P, PACK, HALF], F32) for h in range(2)]
 
-        def residuals(t):
-            nc.vector.tensor_tensor(gap[t][:], rate[t][:], spk_t[t][:], ALU.subtract)
-            nc.vector.tensor_tensor(ndev[t][:], gap[t][:], rsq[t][:], ALU.mult)
+        def fetch(h):
+            for t in range(PACK):
+                window = dev[t][:].indirect(nb_t[:, HALF_COLS * h : HALF_COLS * (h + 1)])
+                nc.scalar.activation(fetched[h][:, t, :], window, ACT.Copy)
 
-        def likelihood(t):
-            nc.vector.tensor_tensor(nprod[t][:], ntanh[t][:], spk_t[t][:], ALU.mult)
-            for c in range(CHUNKS):
-                add_turned(c, t, rate[t][:, P * c : P * (c + 1)], start=(t == 0))
-            for c in range(CHUNKS):
-                add_turned(c, t, nprod[t][:, P * c : P * (c + 1)])
-
-        scores(0)
-        for t in range(1, TILES):
-            prepare(t, nc.scalar.copy if t == 1 else nc.vector.tensor_copy)
-            scores(t)
-        for t in range(TILES):
-            residuals(t)
-            likelihood(t)
-
-        w_bf = sbuf("w_bf", [P, N, PACK], BF16)
-        w_codes = sbuf("w_codes", [P, N], U32)
-        w_scales = sbuf("w_scales", [P, N], U8)
-
-        def fetch(t, h):
-            window = ndev[t][:].indirect(nb_t[:, HALF_COLS * h : HALF_COLS * (h + 1)])
-            if (t, h) == (TILES - 1, 0):
-                nc.vector.tensor_copy(fetched[t][h][:], window)
-            else:
-                nc.scalar.activation(fetched[t][h][:], window, ACT.Copy)
-            for cc in range(2):
-                add_turned(2 * h + cc, t, fetched[t][h][:, P * cc : P * (cc + 1)], stop=(t == TILES - 1))
-
-        def finish(h):
-            words = banks.tile([P, 2, 2, P], F32, name="words", tag="bank")
-            for cc in range(2):
-                c = 2 * h + cc
-                hid_t = sbuf(f"hid_t{c}", [P, H], BF16)
-                nc.vector.tensor_tensor(
-                    hid_t[:].rearrange("p (u m e) -> p u m e", u=2, e=2),
-                    acc[c][:].rearrange("p (m u e) -> p u m e", u=2, e=2),
-                    nunit[:].rearrange("p (u m e) -> p u m e", u=2, e=2),
-                    ALU.mult,
-                )
-                for u in range(2):
-                    nc.tensor.transpose(
-                        words[:, cc, u, :], hid_t[:].bitcast(F32)[:, P * u : P * (u + 1)], ident[:]
-                    )
-            hid_bf = sbuf(f"hid_bf{h}", [P, HALF, PACK], BF16)
-            nc.scalar.copy(
-                hid_bf[:].rearrange("p j r -> p (j r)").bitcast(F32).rearrange("p (c j u) -> p c j u", c=2, u=2),
-                words[:].rearrange("p c u j -> p c j u"),
+        def finish(first, width):
+            h, at = divmod(first, HALF)
+            hid_bf = sbuf(f"hid_bf{first}", [P, width, PACK], BF16)
+            nc.vector.tensor_tensor(
+                hid_bf[:].rearrange("p (c i) t -> p c t i", i=4),
+                fetched[h][:, :, at : at + width].rearrange("p t (c i) -> p c t i", i=4),
+                nll[:, :, first : first + width].rearrange("p t (c i) -> p c t i", i=4),
+                ALU.subtract,
             )
-            hid_codes = sbuf(f"hid_codes{h}", [P, HALF], U32)
-            hid_scales = sbuf(f"hid_scales{h}", [P, HALF], U8)
-            quantize(hid_codes, hid_scales, hid_bf)
-            res = banks.tile([P, 2, HALF], F32, name="res", tag="bank")
+            hid_codes = sbuf(f"hid_codes{first}", [P, width], U32)
+            hid_scales = sbuf(f"hid_scales{first}", [P, width], U8)
+            quantize(hid_codes[:], hid_scales[:], hid_bf[:].rearrange("p j t -> p (j t)"))
+            res = banks.tile([P, 2, width], F32, name=f"res{first}")
             for a in range(2):
                 nc.tensor.matmul_mx(
                     out=res[:, a, :],
@@ -223,17 +164,14 @@ def tile_picked_yplcel_ll_p_kernel(
                     rhs=hid_codes[:].bitcast(FP8X4), rhs_scale=hid_scales[:],
                     start=True, stop=True,
                 )
-            staged = sbuf(f"staged{h}", [P, 2, HALF], F32)
+            staged = sbuf(f"staged{first}", [P, 2, width], F32)
             nc.scalar.copy(staged[:], res[:])
             nc.sync.dma_start(
-                out.rearrange("(a p) j -> p a j", a=2)[:, :, HALF * h : HALF * (h + 1)], staged[:]
+                out.rearrange("(a p) j -> p a j", a=2)[:, :, first : first + width], staged[:]
             )
 
-        for t in range(TILES):
-            fetch(t, 0)
-        interleave(nc.vector.tensor_copy, w_bf, w_raw[:])
-        quantize(w_codes, w_scales, w_bf)
-        for t in range(TILES):
-            fetch(t, 1)
-        finish(0)
-        finish(1)
+        fetch(0)
+        fetch(1)
+        finish(0, HALF)
+        finish(HALF, HALF // 2)
+        finish(HALF + HALF // 2, HALF // 2)

@@ -54,23 +54,23 @@ def tile_picked_yplcel_ll_p_kernel(
         spk_rows = spk.rearrange("(p t) j -> p t j", t=PACK)
 
         nc.gpsimd.memset(xs[:].bitcast(I32), 0)
+        nc.sync.dma_start(h_raw[0][:], hT_rows[:, :, : H // 2])
         nc.sync.dma_start(offs_t[:], offs)
         for q in range(4):
             nc.sync.dma_start(
                 xs[32 * q : 32 * q + 4, :].bitcast(I32),
                 x_scales[0, 4 * q : 4 * q + 4, :].bitcast(I32),
             )
-        for a in range(2):
-            nc.sync.dma_start(h_raw[a][:], hT_rows[:, :, H // 2 * a : H // 2 * (a + 1)])
+        nc.sync.dma_start(h_raw[1][:], hT_rows[:, :, H // 2 :])
         nc.sync.dma_start(
             xw[:].bitcast(I32), x_words[0].rearrange("p n r -> p (n r)").bitcast(I32)
         )
-        nc.sync.dma_start(w_raw[:], w1.rearrange("(p r) n -> p r n", r=PACK))
         nc.sync.dma_start(spk_t[0][:], spk_rows[:, 0, :])
         nc.sync.dma_start(u_t[:], unit.rearrange("(p t) o -> p (t o)", t=PACK))
         for t in range(1, PACK):
             nc.sync.dma_start(spk_t[t][:], spk_rows[:, t, :])
         nc.sync.dma_start(nb_t[:], nb)
+        nc.sync.dma_start(w_raw[:], w1.rearrange("(p r) n -> p r n", r=PACK))
 
         gs = sbuf("gs", [P, S], U8)
         gw = [sbuf(f"gw{h}", [P, HALF], U32) for h in range(2)]
@@ -98,8 +98,6 @@ def tile_picked_yplcel_ll_p_kernel(
         w_bf = sbuf("w_bf", [P, N, PACK], BF16)
         w_codes = sbuf("w_codes", [P, N], U32)
         w_scales = sbuf("w_scales", [P, N], U8)
-        interleave(nc.vector.tensor_copy, w_bf, w_raw)
-        quantize(w_codes[:], w_scales[:], w_bf[:].rearrange("p n r -> p (n r)"))
 
         tanh = [sbuf(f"tanh{t}", [P, S], F32) for t in range(PACK)]
         rate = [sbuf(f"rate{t}", [P, S], F32) for t in range(PACK)]
@@ -129,26 +127,36 @@ def tile_picked_yplcel_ll_p_kernel(
             if t > 0:
                 rates(t, y, slice(0, S))
 
-        for t in range(PACK):
+        def terms(t, cols):
             u = u_t[:, t : t + 1]
-            nc.vector.scalar_tensor_tensor(prod[t][:], tanh[t][:], u, spk_t[t][:], ALU.mult, ALU.mult)
-            nc.vector.tensor_tensor(gap[t][:], spk_t[t][:], rate[t][:], ALU.subtract)
-            nc.vector.scalar_tensor_tensor(nll[:, t, :], rate[t][:], u, prod[t][:], ALU.mult, ALU.subtract)
-            nc.vector.scalar_tensor_tensor(dev[t][:], gap[t][:], u, rsq[t][:], ALU.mult, ALU.mult)
+            nc.vector.tensor_tensor(gap[t][:, cols], spk_t[t][:, cols], rate[t][:, cols], ALU.subtract)
+            nc.vector.scalar_tensor_tensor(
+                prod[t][:, cols], tanh[t][:, cols], u, spk_t[t][:, cols], ALU.mult, ALU.mult
+            )
+            nc.vector.scalar_tensor_tensor(
+                dev[t][:, cols], gap[t][:, cols], u, rsq[t][:, cols], ALU.mult, ALU.mult
+            )
+            nc.vector.scalar_tensor_tensor(
+                nll[:, t, cols], rate[t][:, cols], u, prod[t][:, cols], ALU.mult, ALU.subtract
+            )
 
-        fetched = [sbuf(f"fetched{h}", [P, PACK, HALF], F32) for h in range(2)]
+        terms(0, slice(0, HALF))
+        terms(0, slice(HALF, S))
+        for t in range(1, PACK):
+            terms(t, slice(0, S))
 
-        def fetch(h):
+        def fetch(first, width, tag):
+            fetched = keep.tile([P, PACK, width], F32, name=f"fetched{first}", tag=tag, align_bytes=64)
             for t in range(PACK):
-                window = dev[t][:].indirect(nb_t[:, HALF_COLS * h : HALF_COLS * (h + 1)])
-                nc.scalar.activation(fetched[h][:, t, :], window, ACT.Copy)
+                window = dev[t][:].indirect(nb_t[:, first // 16 : (first + width) // 16])
+                nc.scalar.activation(fetched[:, t, :], window, ACT.Copy)
+            return fetched
 
-        def finish(first, width):
-            h, at = divmod(first, HALF)
+        def finish(first, width, fetched, copy):
             hid_bf = sbuf(f"hid_bf{first}", [P, width, PACK], BF16)
             nc.vector.tensor_tensor(
                 hid_bf[:].rearrange("p (c i) t -> p c t i", i=4),
-                fetched[h][:, :, at : at + width].rearrange("p t (c i) -> p c t i", i=4),
+                fetched[:].rearrange("p t (c i) -> p c t i", i=4),
                 nll[:, :, first : first + width].rearrange("p t (c i) -> p c t i", i=4),
                 ALU.subtract,
             )
@@ -165,13 +173,18 @@ def tile_picked_yplcel_ll_p_kernel(
                     start=True, stop=True,
                 )
             staged = sbuf(f"staged{first}", [P, 2, width], F32)
-            nc.scalar.copy(staged[:], res[:])
+            copy(staged[:], res[:])
             nc.sync.dma_start(
                 out.rearrange("(a p) j -> p a j", a=2)[:, :, first : first + width], staged[:]
             )
 
-        fetch(0)
-        fetch(1)
-        finish(0, HALF)
-        finish(HALF, HALF // 2)
-        finish(HALF + HALF // 2, HALF // 2)
+        interleave(nc.scalar.copy, w_bf, w_raw)
+        quantize(w_codes[:], w_scales[:], w_bf[:].rearrange("p n r -> p (n r)"))
+        pieces = (
+            (0, HALF, "fetched0", nc.scalar.copy),
+            (HALF, HALF // 2, f"gap{PACK - 1}", nc.scalar.copy),
+            (HALF + HALF // 2, HALF // 2, f"rsq{PACK - 1}", nc.vector.tensor_copy),
+        )
+        found = [fetch(first, width, tag) for first, width, tag, copy in pieces]
+        for (first, width, tag, copy), fetched in zip(pieces, found):
+            finish(first, width, fetched, copy)

@@ -46,29 +46,29 @@ def tile_picked_yplcel_ll_p_kernel(
         nb_t = keep.tile([P, S // 16], U16, name="nb_t")
         xs = sbuf("xs", [P, T], U8)
         xw = keep.tile([P, T], U32, name="xw", tag="words", align_bytes=64)
-        h_raw = [sbuf(f"h_raw{a}", [P, PACK, H // 2], F32) for a in range(2)]
-        spk_t = [sbuf(f"spk{t}", [P, S], F32) for t in range(PACK)]
+        h_raw = [sbuf(f"h_raw{a}", [P, 2, H], F32) for a in range(2)]
+        spk_pair = [sbuf(f"spk{a}", [P, 2, S], F32) for a in range(2)]
+        spk_t = [spk_pair[t // 2][:, t % 2, :] for t in range(PACK)]
         u_t = sbuf("u_t", [P, PACK], F32)
         w_raw = sbuf("w_raw", [P, PACK, N], F32)
         hT_rows = hT.rearrange("(p r) c -> p r c", r=PACK)
         spk_rows = spk.rearrange("(p t) j -> p t j", t=PACK)
 
         nc.gpsimd.memset(xs[:].bitcast(I32), 0)
-        nc.sync.dma_start(h_raw[0][:], hT_rows[:, :, : H // 2])
+        nc.sync.dma_start(h_raw[0][:], hT_rows[:, :2, :])
         nc.sync.dma_start(offs_t[:], offs)
         for q in range(4):
             nc.sync.dma_start(
                 xs[32 * q : 32 * q + 4, :].bitcast(I32),
                 x_scales[0, 4 * q : 4 * q + 4, :].bitcast(I32),
             )
-        nc.sync.dma_start(h_raw[1][:], hT_rows[:, :, H // 2 :])
+        nc.sync.dma_start(h_raw[1][:], hT_rows[:, 2:, :])
         nc.sync.dma_start(
             xw[:].bitcast(I32), x_words[0].rearrange("p n r -> p (n r)").bitcast(I32)
         )
-        nc.sync.dma_start(spk_t[0][:], spk_rows[:, 0, :])
+        nc.sync.dma_start(spk_pair[0][:], spk_rows[:, :2, :])
         nc.sync.dma_start(u_t[:], unit.rearrange("(p t) o -> p (t o)", t=PACK))
-        for t in range(1, PACK):
-            nc.sync.dma_start(spk_t[t][:], spk_rows[:, t, :])
+        nc.sync.dma_start(spk_pair[1][:], spk_rows[:, 2:, :])
         nc.sync.dma_start(nb_t[:], nb)
         nc.sync.dma_start(w_raw[:], w1.rearrange("(p r) n -> p r n", r=PACK))
 
@@ -79,11 +79,12 @@ def tile_picked_yplcel_ll_p_kernel(
         first_scales = sbuf("first_scales", [P, P], U8)
 
         nc.vector.tensor_copy(gs[:], xs[:].indirect(offs_t[:]))
-        for a, copy in enumerate((nc.scalar.copy, nc.vector.tensor_copy)):
-            copy(
-                h_bf[:, :, P // 2 * a : P // 2 * (a + 1), :].rearrange("p t m r -> p m r t"),
-                h_raw[a][:].rearrange("p r (m t) -> p m r t", t=PACK),
-            )
+        for a in range(2):
+            for first, copy in ((0, nc.vector.tensor_copy), (2, nc.scalar.copy)):
+                copy(
+                    h_bf[:, first : first + 2, :, 2 * a : 2 * (a + 1)].rearrange("p t m r -> p m r t"),
+                    h_raw[a][:].rearrange("p r (m t) -> p m r t", t=PACK)[:, :, :, first : first + 2],
+                )
         quantize(first_codes[:], first_scales[:], h_bf[:, 0].rearrange("p m r -> p (m r)"))
         for h in range(2):
             nc.vector.tensor_copy(

from contextlib import ExitStack

import concourse.mybir as mybir

K, T, S, N, H = 512, 1024, 512, 256, 512
FLOPS = 2 * K * H * S + 2 * H * N * S

F32 = mybir.dt.float32
BF16 = mybir.dt.bfloat16
I32 = mybir.dt.int32
U32 = mybir.dt.uint32
U16 = mybir.dt.uint16
U8 = mybir.dt.uint8
FP8X4 = mybir.dt.float8_e4m3fn_x4
ACT = mybir.ActivationFunctionType
ALU = mybir.AluOpType

P = 128
PACK = 4
HALF = S // 2
HALF_COLS = HALF // 16


def interleave(copy, grouped, raw):
    copy(
        grouped[:].rearrange("p (c i) r -> p c r i", i=4),
        raw[:].rearrange("p r (c i) -> p c r i", i=4),
    )


def tile_picked_yplcel_ll_p_kernel(
    tc, x_words, x_scales, hT, spk, unit, w1, offs, nb, out
):
    nc = tc.nc
    with ExitStack() as ctx:
        keep = ctx.enter_context(tc.tile_pool(name="keep", bufs=1))
        banks = ctx.enter_context(tc.psum_pool(name="banks", bufs=1))

        def sbuf(name, shape, dtype):
            return keep.tile(shape, dtype, name=name, align_bytes=64)

        def quantize(codes, scales, grouped):
            nc.vector.quantize_mx(out=codes.bitcast(FP8X4), scales=scales, in_=grouped)

        offs_t = keep.tile([P, S // 16], U16, name="offs_t")
        nb_t = keep.tile([P, S // 16], U16, name="nb_t")
        xs = sbuf("xs", [P, T], U8)
        xw = keep.tile([P, T], U32, name="xw", tag="words", align_bytes=64)
        h_raw = [sbuf(f"h_raw{a}", [P, 2, H], F32) for a in range(2)]
        spk_pair = [sbuf(f"spk{a}", [P, 2, S], F32) for a in range(2)]
        spk_t = [spk_pair[t // 2][:, t % 2, :] for t in range(PACK)]
        u_t = sbuf("u_t", [P, PACK], F32)
        w_raw = sbuf("w_raw", [P, PACK, N], F32)
        hT_rows = hT.rearrange("(p r) c -> p r c", r=PACK)
        spk_rows = spk.rearrange("(p t) j -> p t j", t=PACK)

        nc.gpsimd.memset(xs[:].bitcast(I32), 0)
        nc.sync.dma_start(h_raw[0][:], hT_rows[:, :2, :])
        nc.sync.dma_start(offs_t[:], offs)
        for q in range(4):
            nc.sync.dma_start(
                xs[32 * q : 32 * q + 4, :].bitcast(I32),
                x_scales[0, 4 * q : 4 * q + 4, :].bitcast(I32),
            )
        nc.sync.dma_start(h_raw[1][:], hT_rows[:, 2:, :])
        nc.sync.dma_start(
            xw[:].bitcast(I32), x_words[0].rearrange("p n r -> p (n r)").bitcast(I32)
        )
        nc.sync.dma_start(spk_pair[0][:], spk_rows[:, :2, :])
        nc.sync.dma_start(u_t[:], unit.rearrange("(p t) o -> p (t o)", t=PACK))
        nc.sync.dma_start(spk_pair[1][:], spk_rows[:, 2:, :])
        nc.sync.dma_start(nb_t[:], nb)
        nc.sync.dma_start(w_raw[:], w1.rearrange("(p r) n -> p r n", r=PACK))

        gs = sbuf("gs", [P, S], U8)
        gw = [sbuf(f"gw{h}", [P, HALF], U32) for h in range(2)]
        h_bf = sbuf("h_bf", [P, PACK, P, PACK], BF16)
        first_codes = sbuf("first_codes", [P, P], U32)
        first_scales = sbuf("first_scales", [P, P], U8)

        nc.vector.tensor_copy(gs[:], xs[:].indirect(offs_t[:]))
        for a in range(2):
            for first, copy in ((0, nc.vector.tensor_copy), (2, nc.scalar.copy)):
                copy(
                    h_bf[:, first : first + 2, :, 2 * a : 2 * (a + 1)].rearrange("p t m r -> p m r t"),
                    h_raw[a][:].rearrange("p r (m t) -> p m r t", t=PACK)[:, :, :, first : first + 2],
                )
        quantize(first_codes[:], first_scales[:], h_bf[:, 0].rearrange("p m r -> p (m r)"))
        for h in range(2):
            nc.vector.tensor_copy(
                gw[h][:], xw[:].indirect(offs_t[:, HALF_COLS * h : HALF_COLS * (h + 1)])
            )
        rest_codes = keep.tile([P, H - P], U32, name="rest_codes", tag="words", align_bytes=64)
        rest_scales = sbuf("rest_scales", [P, H - P], U8)
        quantize(rest_codes[:], rest_scales[:], h_bf[:, 1:].rearrange("p t m r -> p (t m r)"))
        h_codes = [first_codes[:]] + [rest_codes[:, P * t : P * (t + 1)] for t in range(PACK - 1)]
        h_scales = [first_scales[:]] + [rest_scales[:, P * t : P * (t + 1)] for t in range(PACK - 1)]

        w_bf = sbuf("w_bf", [P, N, PACK], BF16)
        w_codes = sbuf("w_codes", [P, N], U32)
        w_scales = sbuf("w_scales", [P, N], U8)

        tanh = [sbuf(f"tanh{t}", [P, S], F32) for t in range(PACK)]
        rate = [sbuf(f"rate{t}", [P, S], F32) for t in range(PACK)]
        rsq = [sbuf(f"rsq{t}", [P, S], F32) for t in range(PACK)]
        gap = [sbuf(f"gap{t}", [P, S], F32) for t in range(PACK)]
        dev = [sbuf(f"dev{t}", [P, S], F32) for t in range(PACK)]
        prod = [sbuf(f"prod{t}", [P, S], F32) for t in range(PACK)]
        nll = sbuf("nll", [P, PACK, S], F32)

        def rates(t, y, cols):
            nc.scalar.activation(tanh[t][:, cols], y[:, cols], ACT.Tanh)
            nc.scalar.activation(rate[t][:, cols], tanh[t][:, cols], ACT.Exp)
            nc.scalar.activation(rsq[t][:, cols], tanh[t][:, cols], ACT.Exp, scale=-0.5)

        for t in range(PACK):
            y = banks.tile([P, S], F32, name=f"y{t}")
            for h in range(2):
                cols = slice(HALF * h, HALF * (h + 1))
                nc.tensor.matmul_mx(
                    out=y[:, cols],
                    lhsT=h_codes[t].bitcast(FP8X4), lhsT_scale=h_scales[t],
                    rhs=gw[h][:].bitcast(FP8X4), rhs_scale=gs[:, cols],
                    start=True, stop=True,
                )
                if t == 0:
                    rates(t, y, cols)
            if t > 0:
                rates(t, y, slice(0, S))

        def terms(t, cols):
            u = u_t[:, t : t + 1]
            nc.vector.tensor_tensor(gap[t][:, cols], spk_t[t][:, cols], rate[t][:, cols], ALU.subtract)
            nc.vector.scalar_tensor_tensor(
                prod[t][:, cols], tanh[t][:, cols], u, spk_t[t][:, cols], ALU.mult, ALU.mult
            )
            nc.vector.scalar_tensor_tensor(
                dev[t][:, cols], gap[t][:, cols], u, rsq[t][:, cols], ALU.mult, ALU.mult
            )
            nc.vector.scalar_tensor_tensor(
                nll[:, t, cols], rate[t][:, cols], u, prod[t][:, cols], ALU.mult, ALU.subtract
            )

        terms(0, slice(0, HALF))
        terms(0, slice(HALF, S))
        for t in range(1, PACK):
            terms(t, slice(0, S))

        def fetch(first, width, tag):
            fetched = keep.tile([P, PACK, width], F32, name=f"fetched{first}", tag=tag, align_bytes=64)
            for t in range(PACK):
                window = dev[t][:].indirect(nb_t[:, first // 16 : (first + width) // 16])
                nc.scalar.activation(fetched[:, t, :], window, ACT.Copy)
            return fetched

        def finish(first, width, fetched, copy):
            hid_bf = sbuf(f"hid_bf{first}", [P, width, PACK], BF16)
            nc.vector.tensor_tensor(
                hid_bf[:].rearrange("p (c i) t -> p c t i", i=4),
                fetched[:].rearrange("p t (c i) -> p c t i", i=4),
                nll[:, :, first : first + width].rearrange("p t (c i) -> p c t i", i=4),
                ALU.subtract,
            )
            hid_codes = sbuf(f"hid_codes{first}", [P, width], U32)
            hid_scales = sbuf(f"hid_scales{first}", [P, width], U8)
            quantize(hid_codes[:], hid_scales[:], hid_bf[:].rearrange("p j t -> p (j t)"))
            res = banks.tile([P, 2, width], F32, name=f"res{first}")
            for a in range(2):
                nc.tensor.matmul_mx(
                    out=res[:, a, :],
                    lhsT=w_codes[:, P * a : P * (a + 1)].bitcast(FP8X4),
                    lhsT_scale=w_scales[:, P * a : P * (a + 1)],
                    rhs=hid_codes[:].bitcast(FP8X4), rhs_scale=hid_scales[:],
                    start=True, stop=True,
                )
            staged = sbuf(f"staged{first}", [P, 2, width], F32)
            copy(staged[:], res[:])
            nc.sync.dma_start(
                out.rearrange("(a p) j -> p a j", a=2)[:, :, first : first + width], staged[:]
            )

        interleave(nc.scalar.copy, w_bf, w_raw)
        quantize(w_codes[:], w_scales[:], w_bf[:].rearrange("p n r -> p (n r)"))
        pieces = (
            (0, HALF, "fetched0", nc.scalar.copy),
            (HALF, HALF // 2, f"gap{PACK - 1}", nc.scalar.copy),
            (HALF + HALF // 2, HALF // 2, f"rsq{PACK - 1}", nc.vector.tensor_copy),
        )
        found = [fetch(first, width, tag) for first, width, tag, copy in pieces]
        for (first, width, tag, copy), fetched in zip(pieces, found):
            finish(first, width, fetched, copy)
